import numpy as np
import ml_dtypes


def mxq(x, axis, fmt="e4m3"):
    dtype, down = {"e4m3": (ml_dtypes.float8_e4m3fn, 7), "e5m2": (ml_dtypes.float8_e5m2, 14)}[fmt]
    v = np.moveaxis(np.asarray(x, np.float32).astype(ml_dtypes.bfloat16).astype(np.float64), axis, -1)
    blocks = v.reshape(v.shape[:-1] + (-1, 32))
    amax = np.abs(blocks).max(-1, keepdims=True)
    byte = np.maximum(np.where(amax > 0, np.frexp(amax)[1] - 1 + 127, 0) - down, 1)
    scale = np.exp2(byte - 127.0)
    codes = (blocks / scale).astype(np.float32).astype(dtype).astype(np.float64)
    return np.moveaxis((codes * scale).reshape(v.shape), -1, axis)


WIDE = False


def mx_kscale(k):
    if not WIDE:
        return np.ones(k)
    levels = np.array([10, -10, 5, -5, 0])
    if k % 512:
        return np.exp2(np.random.permutation(np.resize(levels, k // 32))).repeat(32)
    a = np.empty((k // 512, 16))
    for p in range(k // 512):
        a[p, :8] = np.random.permutation(np.resize(levels, 8))
        for g in range(8):
            far = levels[np.abs(levels - a[p, g]) >= 10]
            a[p, g + 8] = far[np.random.randint(len(far))]
    return np.exp2(a.ravel()).repeat(32)


def f64(x):
    return np.asarray(x).astype(np.float64)


def striped(idx):
    return np.tile(idx.reshape(-1, 16).T, (8, 1)).astype(np.uint16)


def unstriped(offs):
    return offs[:16].T.reshape(-1).astype(np.int64)


def striped8(idx):
    return np.concatenate([x.reshape(-1, 16).T for x in idx]).astype(np.uint16)


def runs(offs, k):
    lists = np.stack([offs[16 * r : 16 * r + 16].T.reshape(-1) for r in range(8)]).astype(np.int64)
    return lists[np.arange(k) % 512 // 64]


def pack_weight(w):
    k, n = w.shape
    w = f64(np.asarray(w, np.float32).astype(ml_dtypes.bfloat16)).reshape(k // 32, 32, n)
    amax = np.abs(w).max(1)
    byte = np.clip(np.where(amax > 0, np.frexp(amax)[1] - 1 + 127 - 7, 1), 1, 254)
    scaled = (w * np.exp2(127.0 - byte)[:, None, :]).reshape(k, n).astype(np.float32)
    words = np.ascontiguousarray(scaled.reshape(k // 512, 128, 4, n).transpose(0, 1, 3, 2)).astype(ml_dtypes.float8_e4m3fn).view(np.uint8)
    return words, np.ascontiguousarray(byte.astype(np.uint8).reshape(k // 512, 16, n))


def unpack_weight(words, scales):
    g, p, n, _ = words.shape
    vals = np.ascontiguousarray(words).view(ml_dtypes.float8_e4m3fn).astype(np.float64) * np.repeat(np.exp2(scales.astype(np.float64) - 127.0), 8, axis=1)[..., None]
    return vals.transpose(0, 1, 3, 2).reshape(g * 512, n)


E2M1 = np.array([0.0, 0.5, 1.0, 1.5, 2.0, 3.0, 4.0, 6.0, -0.0, -0.5, -1.0, -1.5, -2.0, -3.0, -4.0, -6.0])


def pack_fp4(w):
    k, n = w.shape
    w = f64(np.asarray(w, np.float32).astype(ml_dtypes.bfloat16)).reshape(k // 32, 32, n)
    amax = np.abs(w).max(1)
    mant, ex = np.frexp(amax / 6.0)
    byte = np.clip(np.where(amax > 0, np.where(mant > 0.5, ex, ex - 1) + 127, 1), 1, 254)
    scaled = (w * np.exp2(127.0 - byte)[:, None, :]).reshape(k, n).astype(np.float32)
    c = np.ascontiguousarray(scaled.reshape(k // 512, 128, 4, n).transpose(0, 1, 3, 2)).astype(ml_dtypes.float4_e2m1fn).view(np.uint8) & 0xF
    words = (c[..., 0::2] | (c[..., 1::2] << 4)).reshape(k // 512, 128, 2 * n)
    return np.ascontiguousarray(words), np.ascontiguousarray(byte.astype(np.uint8).reshape(k // 512, 16, n))


def unpack_fp4(words, scales):
    g, _, n = scales.shape
    words = np.ascontiguousarray(words).reshape(g, 128, n, 2)
    nib = np.empty((g, 128, n, 4), np.uint8)
    nib[..., 0::2] = words & 0xF
    nib[..., 1::2] = words >> 4
    vals = E2M1[nib] * np.repeat(np.exp2(scales.astype(np.float64) - 127.0), 8, axis=1)[..., None]
    return vals.transpose(0, 1, 3, 2).reshape(g * 512, n)


def sigmoid(v):
    return 1.0 / (1.0 + np.exp(-np.maximum(v, -700.0)))

def planes(y):
    n, m = y.shape
    v = y.astype(np.float32).astype(ml_dtypes.bfloat16).astype(np.float64).reshape(n // 32, 32, m)
    top = np.abs(v).max(1)
    byte = np.clip(np.where(top > 0, np.frexp(top)[1] - 1 + 127 - 7, 1), 1, 254)
    codes = (v * np.exp2(127.0 - byte)[:, None, :]).reshape(n, m).astype(np.float32).astype(ml_dtypes.float8_e4m3fn).view(np.uint8)
    words = codes.reshape(n // 512, 128, 4, m).transpose(0, 1, 3, 2)
    return np.ascontiguousarray(words), np.ascontiguousarray(byte.astype(np.uint8).reshape(n // 512, 16, m))


K, T, S, N, G, H, U = 512, 2048, 512, 512, 2048, 512, 1024


def setup_inputs():
    n = np.random.standard_normal
    s = mx_kscale(K)[:, None]
    u = mx_kscale(S)
    packed_xT = pack_weight(n((K, T)) * s)
    packed_dT = pack_weight(n((K, G)) / s)
    packed_w1 = pack_fp4(n((H, N)) / np.sqrt(H) / u[:, None])
    return {
        "x_words": packed_xT[0],
        "x_scales": packed_xT[1],
        "d_words": packed_dT[0],
        "d_scales": packed_dT[1],
        "gn": (np.random.uniform(0.5, 1.5, (H, 1)) * u[:, None]).astype(np.float32),
        "w1_words": packed_w1[0],
        "w1_scales": packed_w1[1],
        "mem": n((N, U)).astype(np.float32),
        "offs": striped(np.random.permutation(T)[:S]),
        "kidx": striped8(np.random.randint(0, G, (8, H))),
        "n1": striped8(np.stack([np.random.permutation(S) for _ in range(8)])),
        "n2": striped8(np.stack([np.random.permutation(S) for _ in range(8)])),
        "n3": striped8(np.stack([np.random.permutation(U)[:S] for _ in range(8)])),
    }


def reference(x_words, x_scales, d_words, d_scales, gn, w1_words, w1_scales, mem, offs, kidx, n1, n2, n3):
    old = f64(mem)[np.arange(N)[:, None], runs(n3, N)]
    d_kidx = unpack_weight(d_words, d_scales)[np.arange(K)[:, None], runs(kidx, K)]
    xq = unpack_weight(x_words, x_scales)[:, unstriped(offs)]
    s = 0.0625 * (d_kidx.T @ xq)
    ex = np.exp(0.5 * s)
    z = f64(gn) * ((2.0 * ex) / (ex + ex[np.arange(H)[:, None], runs(n1, H)] + ex[np.arange(H)[:, None], runs(n2, H)]))
    h = unpack_fp4(w1_words, w1_scales).T @ mxq(z, 0, "e4m3")
    nw = old + sigmoid(h) * (h - old)
    out = f64(mem).copy()
    out[np.arange(N)[:, None], runs(n3, N)] = nw
    return (out,) + planes(out)

@@ -1,0 +1,220 @@
+from contextlib import ExitStack
+
+import concourse.mybir as mybir
+
+F32 = mybir.dt.float32
+BF16 = mybir.dt.bfloat16
+I32 = mybir.dt.int32
+U32 = mybir.dt.uint32
+U16 = mybir.dt.uint16
+U8 = mybir.dt.uint8
+FP8X4 = mybir.dt.float8_e4m3fn_x4
+FP4X4 = mybir.dt.float4_e2m1fn_x4
+ACT = mybir.ActivationFunctionType
+ALU = mybir.AluOpType
+
+P = 128
+PACK = 4
+TABLE = 2048
+S = 512
+SLOTS = 1024
+HALF = S // 2
+SCORE = 0.0625 * 0.5
+FLOPS = 2 * 2 * 512 * 512 * 512
+
+
+def tile_picked_keysharepaget_none_po_kernel(
+    tc, x_words, x_scales, d_words, d_scales, gn, w1_words, w1_scales, mem,
+    offs, kidx, n1, n2, n3, out_0, out_1, out_2,
+):
+    nc = tc.nc
+    with ExitStack() as ctx:
+        keep = ctx.enter_context(tc.tile_pool(name="keep", bufs=1))
+        psum = ctx.enter_context(tc.psum_pool(name="psum", bufs=1))
+
+        def sb(name, shape, dtype, after=None):
+            return keep.tile(shape, dtype, name=name, tag=after or name, align_bytes=64)
+
+        kidx_t = sb("kidx_t", [P, S // 16], U16)
+        offs_t = sb("offs_t", [P, S // 16], U16)
+        n1_t = sb("n1_t", [P, S // 16], U16)
+        n2_t = sb("n2_t", [P, S // 16], U16)
+        n3_t = sb("n3_t", [P, S // 16], U16)
+        d_tab = sb("d_tab", [P, TABLE], I32)
+        x_tab = sb("x_tab", [P, TABLE], I32)
+        ds_tab = sb("ds_tab", [P, TABLE], U8)
+        xs_tab = sb("xs_tab", [P, TABLE], U8)
+        win = [sb("win%d" % t, [P, 2 * S], F32) for t in range(PACK)]
+        warm = sb("warm", [P, 2], F32)
+
+        nc.gpsimd.memset(ds_tab[:].bitcast(I32), 0)
+        nc.vector.memset(xs_tab[:].bitcast(I32), 0)
+        nc.vector.memset(warm[:, 0:1], 0.0)
+        for t in range(PACK):
+            nc.vector.memset(win[t][:, S:], 0.0)
+
+        nc.sync.dma_start(kidx_t[:], kidx)
+        ds_rows = d_scales[0].bitcast(I32)
+        nc.scalar.dma_start(ds_tab[:].bitcast(I32)[0:P:8, :], ds_rows)
+        nc.sync.dma_start(d_tab[:], d_words[0].rearrange("p n t -> p (n t)").bitcast(I32))
+        nc.sync.dma_start(offs_t[:], offs)
+        nc.sync.dma_start(n1_t[:], n1)
+        nc.sync.dma_start(n2_t[:], n2)
+        nc.sync.dma_start(n3_t[:], n3)
+        nc.sync.dma_start(x_tab[:], x_words[0].rearrange("p n t -> p (n t)").bitcast(I32))
+        xs_rows = x_scales[0].bitcast(I32)
+        for q in range(4):
+            nc.gpsimd.dma_start(xs_tab[:].bitcast(I32)[32 * q : 32 * q + 4, :], xs_rows[4 * q : 4 * q + 4, :])
+
+        nc.scalar.activation(warm[:, 1:2], warm[:, 0:1], ACT.Exp)
+
+        ds_got = sb("ds_got", [P, S], U8)
+        ds_dealt = sb("ds_dealt", [P, S], U8)
+        nc.vector.tensor_copy(ds_got[:], ds_tab[:].indirect(kidx_t[:]))
+        nc.vector.tensor_copy(
+            ds_dealt[:].rearrange("p (t m) -> p m t", t=PACK), ds_got[:].rearrange("p (m t) -> p m t", t=PACK)
+        )
+        for j in range(1, 4):
+            nc.scalar.dma_start(ds_dealt[:].bitcast(I32)[j:P:32, :], ds_dealt[:].bitcast(I32)[8 * j : P : 32, :])
+        d_got = sb("d_got", [P, S], U32)
+        d_dealt = sb("d_dealt", [P, S], U32)
+        nc.vector.tensor_copy(d_got[:], d_tab[:].bitcast(U32).indirect(kidx_t[:]))
+        nc.vector.tensor_copy(
+            d_dealt[:].rearrange("p (t m) -> p m t", t=PACK), d_got[:].rearrange("p (m t) -> p m t", t=PACK)
+        )
+        xs_got = sb("xs_got", [P, S], U8)
+        x_got = sb("x_got", [P, S], U32)
+        nc.vector.tensor_copy(xs_got[:], xs_tab[:].indirect(offs_t[:]))
+        nc.vector.tensor_copy(x_got[:], x_tab[:].bitcast(U32).indirect(offs_t[:]))
+
+        mem_rows = mem.rearrange("(p t) u -> p t u", t=PACK)
+        page = [sb("page%d" % t, [P, SLOTS], F32, after=a) for t, a in enumerate(("ds_tab", "d_tab", "xs_tab", "x_tab"))]
+        w_raw = sb("w_raw", [P, 2 * S], U8, after="ds_got")
+        ws_raw = sb("ws_raw", [P, S], U8)
+        gain = sb("gain", [P, PACK], F32, after="d_got")
+        nc.gpsimd.memset(ws_raw[:].bitcast(I32), 0)
+        nc.sync.dma_start(w_raw[:].bitcast(I32), w1_words[0].bitcast(I32))
+        ws_rows = w1_scales[0].bitcast(I32)
+        for q in range(4):
+            nc.gpsimd.dma_start(ws_raw[:].bitcast(I32)[32 * q : 32 * q + 4, :], ws_rows[4 * q : 4 * q + 4, :])
+        nc.sync.dma_start(gain[:], gn.rearrange("(p t) o -> p (t o)", t=PACK))
+        for t in range(PACK):
+            nc.sync.dma_start(page[t][:], mem_rows[:, t, :])
+
+        score = [psum.tile([P, S], F32, name="score%d" % t) for t in range(PACK)]
+        for t in range(PACK):
+            cols = slice(P * t, P * (t + 1))
+            nc.tensor.matmul_mx(
+                out=score[t][:], lhsT=d_dealt[:, cols].bitcast(FP8X4), lhsT_scale=ds_dealt[:, cols],
+                rhs=x_got[:].bitcast(FP8X4), rhs_scale=xs_got[:], start=True, stop=True,
+            )
+
+        w_dealt = sb("w_dealt", [P, 2 * S], U8, after="d_dealt")
+        nc.vector.tensor_copy(
+            w_dealt[:].rearrange("p (t m b) -> p m t b", t=PACK, b=2),
+            w_raw[:].rearrange("p (m t b) -> p m t b", t=PACK, b=2),
+        )
+
+        LAST = PACK - 1
+        first = [sb("first%d" % t, [P, S], F32) for t in range(PACK)]
+        second = sb("second", [P, S], F32)
+        both = [sb("both%d" % t, [P, S], F32) for t in range(PACK)]
+        for t in range(LAST):
+            nc.scalar.activation(win[t][:, :S], score[t][:], ACT.Exp, scale=SCORE)
+        nc.scalar.activation(win[LAST][:, :S], score[LAST][:], ACT.Copy, scale=SCORE)
+        nc.scalar.activation(first[LAST][:], win[LAST][:].indirect(n1_t[:]), ACT.Exp)
+        nc.scalar.activation(second[:], win[LAST][:].indirect(n2_t[:]), ACT.Exp)
+        for t in range(LAST):
+            nc.vector.tensor_copy(first[t][:], win[t][:].indirect(n1_t[:]))
+            nc.vector.tensor_tensor(both[t][:], win[t][:].indirect(n2_t[:]), first[t][:], ALU.add)
+            if t == LAST - 2:
+                nc.vector.tensor_tensor(both[LAST][:], first[LAST][:], second[:], ALU.add)
+        order = [0, 1, 3, 2]
+        logs = sb("logs", [P, PACK, S], F32, after="win3")
+        for t in order:
+            nc.scalar.activation(logs[:, t, :], both[t][:], ACT.Ln)
+        warm2 = sb("warm2", [P, 1], F32)
+        nc.scalar.activation(warm2[:], logs[:, order[-1], 0:1], ACT.Silu)
+        logit = sb("logit", [P, PACK, S], F32)
+        for t in order:
+            nc.vector.scalar_tensor_tensor(logit[:, t, :], score[t][:], SCORE, logs[:, t, :], ALU.mult, ALU.subtract)
+        ws_dealt = sb("ws_dealt", [P, S], U8, after="second")
+        nc.vector.tensor_copy(
+            ws_dealt[:].rearrange("p (t m) -> p m t", t=PACK), ws_raw[:].rearrange("p (m t) -> p m t", t=PACK)
+        )
+        old_m = sb("old_m", [P, S], F32, after="first2")
+        nc.vector.tensor_scalar(old_m[:], page[0][:].indirect(n3_t[:]), -0.5, 0.0, ALU.mult, ALU.add)
+
+        hsum = [psum.tile([P, S], F32, name="hsum%d" % t) for t in range(PACK)]
+        share = [sb("share%d" % a, [P, HALF, PACK], F32, after=("warm2", None)[a]) for a in range(2)]
+        zb = [sb("zb%d" % a, [P, HALF, PACK], BF16) for a in range(2)]
+        z_codes = [sb("z_codes%d" % a, [P, HALF], U32) for a in range(2)]
+        z_scales = [sb("z_scales%d" % a, [P, HALF], U8) for a in range(2)]
+        gain_b = gain[:].unsqueeze(1).broadcast_to([P, HALF, PACK])
+        for a in range(2):
+            cols = slice(HALF * a, HALF * (a + 1))
+            nc.scalar.activation(
+                share[a][:].rearrange("p (c i) t -> p c t i", i=4),
+                logit[:, :, cols].rearrange("p t (c i) -> p c t i", i=4), ACT.Tanh, scale=0.5,
+            )
+        for a in range(2):
+            cols = slice(HALF * a, HALF * (a + 1))
+            nc.vector.scalar_tensor_tensor(zb[a][:], share[a][:], 1.0, gain_b, ALU.add, ALU.mult)
+            nc.vector.quantize_mx(
+                out=z_codes[a][:].bitcast(FP8X4), scales=z_scales[a][:], in_=zb[a][:].rearrange("p j t -> p (j t)")
+            )
+            for t in range(PACK):
+                nc.tensor.matmul_mx(
+                    out=hsum[t][:, cols], lhsT=w_dealt[:, 2 * P * t : 2 * P * (t + 1)].bitcast(FP4X4),
+                    lhsT_scale=ws_dealt[:, P * t : P * (t + 1)],
+                    rhs=z_codes[a][:].bitcast(FP8X4), rhs_scale=z_scales[a][:], start=True, stop=True,
+                )
+
+        out_rows = out_0.rearrange("(p t) u -> p t u", t=PACK)
+        th = [sb("th%d" % t, [P, S], F32) for t in range(PACK)]
+        stay = [sb("stay%d" % t, [P, S], F32) for t in range(PACK)]
+        fresh = [sb("fresh%d" % t, [P, S], F32) for t in range(PACK)]
+        kept = [sb("kept%d" % t, [P, S], F32) for t in range(PACK)]
+        yb = [sb("yb%d" % a, [P, SLOTS // 2, PACK], BF16) for a in range(2)]
+        for a in range(2):
+            cols = slice(HALF * a, HALF * (a + 1))
+            nc.scalar.activation(th[0][:, cols], hsum[0][:, cols], ACT.Tanh, scale=0.5)
+            nc.scalar.activation(fresh[0][:, cols], hsum[0][:, cols], ACT.Silu)
+        for t in range(1, PACK):
+            nc.scalar.activation(th[t][:], hsum[t][:], ACT.Tanh, scale=0.5)
+            nc.scalar.activation(stay[t][:], th[t][:], ACT.Copy, scale=-0.5, bias=0.5)
+            nc.scalar.activation(fresh[t][:], hsum[t][:], ACT.Silu)
+        for t in range(PACK):
+            if t == 0:
+                for a in range(2):
+                    cols = slice(HALF * a, HALF * (a + 1))
+                    nc.vector.scalar_tensor_tensor(kept[0][:, cols], th[0][:, cols], -1.0, old_m[:, cols], ALU.add, ALU.mult)
+                    nc.vector.tensor_tensor(
+                        page[0][:].indirect(n3_t[:, 16 * a : 16 * (a + 1)]), kept[0][:, cols], fresh[0][:, cols], ALU.add
+                    )
+            else:
+                nc.vector.tensor_tensor(kept[t][:], page[t][:].indirect(n3_t[:]), stay[t][:], ALU.mult)
+                nc.vector.tensor_tensor(page[t][:].indirect(n3_t[:]), kept[t][:], fresh[t][:], ALU.add)
+            nc.sync.dma_start(out_rows[:, t, :], page[t][:])
+            for a in range(2):
+                src = page[t][:, a * SLOTS // 2 : (a + 1) * SLOTS // 2]
+                if t == LAST and a == 0:
+                    nc.vector.tensor_copy(yb[a][:, :, t], src)
+                elif t == LAST - 1 and a == 0:
+                    nc.scalar.copy(yb[a][:, :, t:], src.unsqueeze(2).broadcast_to([P, SLOTS // 2, 2]))
+                else:
+                    nc.scalar.copy(yb[a][:, :, t], src)
+
+        y_codes = [sb("y_codes%d" % a, [P, SLOTS // 2], U32) for a in range(2)]
+        y_scales = sb("y_scales", [P, SLOTS], U8)
+        words_out = out_1[0].rearrange("p n t -> p (n t)").bitcast(I32)
+        for a in range(2):
+            cols = slice(a * SLOTS // 2, (a + 1) * SLOTS // 2)
+            nc.vector.quantize_mx(
+                out=y_codes[a][:].bitcast(FP8X4), scales=y_scales[:, cols], in_=yb[a][:].rearrange("p j t -> p (j t)")
+            )
+            nc.sync.dma_start(words_out[:, cols], y_codes[a][:].bitcast(I32))
+        scales_out = out_2[0].bitcast(I32)
+        for q in range(4):
+            eng = nc.scalar if q % 2 else nc.sync
+            eng.dma_start(scales_out[4 * q : 4 * q + 4, :], y_scales[:].bitcast(I32)[32 * q : 32 * q + 4, :])

@@ -19,6 +19,7 @@ TABLE = 2048
 S = 512
 SLOTS = 1024
 HALF = S // 2
+PIECE = S // 4
 SCORE = 0.0625 * 0.5
 FLOPS = 2 * 2 * 512 * 512 * 512
 
@@ -40,76 +41,84 @@ def tile_picked_keysharepaget_none_po_kernel(
         n1_t = sb("n1_t", [P, S // 16], U16)
         n2_t = sb("n2_t", [P, S // 16], U16)
         n3_t = sb("n3_t", [P, S // 16], U16)
-        d_tab = sb("d_tab", [P, TABLE], I32)
-        x_tab = sb("x_tab", [P, TABLE], I32)
         ds_tab = sb("ds_tab", [P, TABLE], U8)
         xs_tab = sb("xs_tab", [P, TABLE], U8)
-        win = [sb("win%d" % t, [P, 2 * S], F32) for t in range(PACK)]
-        warm = sb("warm", [P, 2], F32)
+        win = [sb("win%d" % t, [P, S if t < PACK - 1 else 2 * S], F32) for t in range(PACK)]
+        halves = [(slice(HALF * a, HALF * (a + 1)), slice(16 * a, 16 * (a + 1))) for a in range(2)]
+        warm_in = sb("warm_in", [P, 1], F32)
+        warm = sb("warm", [P, 1], F32)
+        nc.gpsimd.memset(warm_in[:], 0.0)
+        nc.scalar.activation(warm[:], warm_in[:], ACT.Exp)
 
-        nc.gpsimd.memset(ds_tab[:].bitcast(I32), 0)
+        nc.vector.memset(ds_tab[:].bitcast(I32), 0)
         nc.vector.memset(xs_tab[:].bitcast(I32), 0)
-        nc.vector.memset(warm[:, 0:1], 0.0)
-        for t in range(PACK):
-            nc.vector.memset(win[t][:, S:], 0.0)
+        nc.vector.memset(win[PACK - 1][:, S:], 0.0)
 
         nc.sync.dma_start(kidx_t[:], kidx)
         ds_rows = d_scales[0].bitcast(I32)
-        nc.scalar.dma_start(ds_tab[:].bitcast(I32)[0:P:8, :], ds_rows)
-        nc.sync.dma_start(d_tab[:], d_words[0].rearrange("p n t -> p (n t)").bitcast(I32))
+        nc.sync.dma_start(ds_tab[:].bitcast(I32)[0:P:8, :], ds_rows)
+        nc.sync.dma_start(xs_tab[:].bitcast(I32)[0:P:8, :], x_scales[0].bitcast(I32))
         nc.sync.dma_start(offs_t[:], offs)
         nc.sync.dma_start(n1_t[:], n1)
         nc.sync.dma_start(n2_t[:], n2)
         nc.sync.dma_start(n3_t[:], n3)
+        d_tab = sb("d_tab", [P, TABLE], I32, after="warm_in")
+        x_tab = sb("x_tab", [P, TABLE], I32, after="warm")
+        nc.sync.dma_start(d_tab[:], d_words[0].rearrange("p n t -> p (n t)").bitcast(I32))
         nc.sync.dma_start(x_tab[:], x_words[0].rearrange("p n t -> p (n t)").bitcast(I32))
-        xs_rows = x_scales[0].bitcast(I32)
-        for q in range(4):
-            nc.gpsimd.dma_start(xs_tab[:].bitcast(I32)[32 * q : 32 * q + 4, :], xs_rows[4 * q : 4 * q + 4, :])
-
-        nc.scalar.activation(warm[:, 1:2], warm[:, 0:1], ACT.Exp)
-
-        ds_got = sb("ds_got", [P, S], U8)
-        ds_dealt = sb("ds_dealt", [P, S], U8)
-        nc.vector.tensor_copy(ds_got[:], ds_tab[:].indirect(kidx_t[:]))
-        nc.vector.tensor_copy(
-            ds_dealt[:].rearrange("p (t m) -> p m t", t=PACK), ds_got[:].rearrange("p (m t) -> p m t", t=PACK)
-        )
-        for j in range(1, 4):
-            nc.scalar.dma_start(ds_dealt[:].bitcast(I32)[j:P:32, :], ds_dealt[:].bitcast(I32)[8 * j : P : 32, :])
-        d_got = sb("d_got", [P, S], U32)
-        d_dealt = sb("d_dealt", [P, S], U32)
-        nc.vector.tensor_copy(d_got[:], d_tab[:].bitcast(U32).indirect(kidx_t[:]))
-        nc.vector.tensor_copy(
-            d_dealt[:].rearrange("p (t m) -> p m t", t=PACK), d_got[:].rearrange("p (m t) -> p m t", t=PACK)
-        )
-        xs_got = sb("xs_got", [P, S], U8)
-        x_got = sb("x_got", [P, S], U32)
-        nc.vector.tensor_copy(xs_got[:], xs_tab[:].indirect(offs_t[:]))
-        nc.vector.tensor_copy(x_got[:], x_tab[:].bitcast(U32).indirect(offs_t[:]))
-
-        mem_rows = mem.rearrange("(p t) u -> p t u", t=PACK)
-        page = [sb("page%d" % t, [P, SLOTS], F32, after=a) for t, a in enumerate(("ds_tab", "d_tab", "xs_tab", "x_tab"))]
-        w_raw = sb("w_raw", [P, 2 * S], U8, after="ds_got")
+        w_raw = sb("w_raw", [P, 2 * S], U8)
         ws_raw = sb("ws_raw", [P, S], U8)
-        gain = sb("gain", [P, PACK], F32, after="d_got")
+        gain = sb("gain", [P, PACK], F32)
+        nc.gpsimd.dma_start(w_raw[:].bitcast(I32), w1_words[0].bitcast(I32))
         nc.gpsimd.memset(ws_raw[:].bitcast(I32), 0)
-        nc.sync.dma_start(w_raw[:].bitcast(I32), w1_words[0].bitcast(I32))
         ws_rows = w1_scales[0].bitcast(I32)
         for q in range(4):
             nc.gpsimd.dma_start(ws_raw[:].bitcast(I32)[32 * q : 32 * q + 4, :], ws_rows[4 * q : 4 * q + 4, :])
-        nc.sync.dma_start(gain[:], gn.rearrange("(p t) o -> p (t o)", t=PACK))
+        nc.gpsimd.dma_start(gain[:], gn.rearrange("(p t) o -> p (t o)", t=PACK))
+
+
+        ds_got = sb("ds_got", [P, S], U8)
+        xs_got = sb("xs_got", [P, S], U8)
+        planes = sb("planes", [P, 2 * S], U8)
+        nc.vector.tensor_copy(ds_got[:], ds_tab[:].indirect(kidx_t[:]))
+        nc.vector.tensor_copy(xs_got[:], xs_tab[:].indirect(offs_t[:]))
+        nc.vector.tensor_copy(
+            planes[:, :S].rearrange("p (t m) -> p m t", t=PACK), ds_got[:].rearrange("p (m t) -> p m t", t=PACK)
+        )
+        nc.vector.tensor_copy(planes[:, S:].bitcast(I32), xs_got[:].bitcast(I32))
+        for j in range(1, 4):
+            nc.scalar.dma_start(planes[:].bitcast(I32)[j:P:32, :], planes[:].bitcast(I32)[8 * j : P : 32, :])
+        d_got = sb("d_got", [P, S], U32, after="ds_got")
+        d_dealt = sb("d_dealt", [P, S], U32)
+        for cols, ents in halves:
+            nc.vector.tensor_copy(d_got[:, cols], d_tab[:].bitcast(U32).indirect(kidx_t[:, ents]))
+        for a, (cols, ents) in enumerate(halves):
+            nc.vector.tensor_copy(
+                d_dealt[:].rearrange("p (t m) -> p m t", t=PACK)[:, 64 * a : 64 * (a + 1), :],
+                d_got[:, cols].rearrange("p (m t) -> p m t", t=PACK),
+            )
+        x_got = sb("x_got", [P, S], U32)
+        for cols, ents in halves:
+            nc.vector.tensor_copy(x_got[:, cols], x_tab[:].bitcast(U32).indirect(offs_t[:, ents]))
+
+        whole = slice(0, S)
+        parts = [(0, cols) for cols, ents in halves] + [(t, whole) for t in range(1, PACK)]
+        score = []
+        for n, (t, cols) in enumerate(parts):
+            bank = psum.tile([P, S], F32, name="score%d" % n)
+            score.append(bank[:, cols])
+            keys = slice(P * t, P * (t + 1))
+            nc.tensor.matmul_mx(
+                out=score[n], lhsT=d_dealt[:, keys].bitcast(FP8X4), lhsT_scale=planes[:, keys],
+                rhs=x_got[:, cols].bitcast(FP8X4), rhs_scale=planes[:, S:][:, cols], start=True, stop=True,
+            )
+
+        mem_rows = mem.rearrange("(p t) u -> p t u", t=PACK)
+        page = [sb("page%d" % t, [P, SLOTS], F32, after=a) for t, a in enumerate(("warm_in", "ds_got", "x_got", "planes"))]
         for t in range(PACK):
             nc.sync.dma_start(page[t][:], mem_rows[:, t, :])
 
-        score = [psum.tile([P, S], F32, name="score%d" % t) for t in range(PACK)]
-        for t in range(PACK):
-            cols = slice(P * t, P * (t + 1))
-            nc.tensor.matmul_mx(
-                out=score[t][:], lhsT=d_dealt[:, cols].bitcast(FP8X4), lhsT_scale=ds_dealt[:, cols],
-                rhs=x_got[:].bitcast(FP8X4), rhs_scale=xs_got[:], start=True, stop=True,
-            )
-
-        w_dealt = sb("w_dealt", [P, 2 * S], U8, after="d_dealt")
+        w_dealt = sb("w_dealt", [P, 2 * S], U8, after="warm")
         nc.vector.tensor_copy(
             w_dealt[:].rearrange("p (t m b) -> p m t b", t=PACK, b=2),
             w_raw[:].rearrange("p (m t b) -> p m t b", t=PACK, b=2),
@@ -118,57 +127,67 @@ def tile_picked_keysharepaget_none_po_kernel(
         LAST = PACK - 1
         first = [sb("first%d" % t, [P, S], F32) for t in range(PACK)]
         second = sb("second", [P, S], F32)
-        both = [sb("both%d" % t, [P, S], F32) for t in range(PACK)]
-        for t in range(LAST):
-            nc.scalar.activation(win[t][:, :S], score[t][:], ACT.Exp, scale=SCORE)
-        nc.scalar.activation(win[LAST][:, :S], score[LAST][:], ACT.Copy, scale=SCORE)
+        both = {t: sb("both%d" % t, [P, S], F32) for t in (0, 1, LAST)}
+        for n, (t, cols) in enumerate(parts):
+            nc.scalar.activation(win[t][:, cols], score[n], ACT.Exp if t < LAST else ACT.Copy, scale=SCORE)
         nc.scalar.activation(first[LAST][:], win[LAST][:].indirect(n1_t[:]), ACT.Exp)
         nc.scalar.activation(second[:], win[LAST][:].indirect(n2_t[:]), ACT.Exp)
         for t in range(LAST):
-            nc.vector.tensor_copy(first[t][:], win[t][:].indirect(n1_t[:]))
-            nc.vector.tensor_tensor(both[t][:], win[t][:].indirect(n2_t[:]), first[t][:], ALU.add)
-            if t == LAST - 2:
+            for cols, ents in halves:
+                nc.vector.tensor_copy(first[t][:, cols], win[t][:].indirect(n1_t[:, ents]))
+            if t == LAST - 1:
                 nc.vector.tensor_tensor(both[LAST][:], first[LAST][:], second[:], ALU.add)
-        order = [0, 1, 3, 2]
-        logs = sb("logs", [P, PACK, S], F32, after="win3")
-        for t in order:
-            nc.scalar.activation(logs[:, t, :], both[t][:], ACT.Ln)
+                both[t] = sb("both%d" % t, [P, S], F32, after="second")
+            for cols, ents in halves:
+                nc.vector.tensor_tensor(both[t][:, cols], win[t][:].indirect(n2_t[:, ents]), first[t][:, cols], ALU.add)
+        logs_a = sb("logs_a", [P, LAST, S], F32, after="win3")
+        logs_b = sb("logs_b", [P, S], F32)
+        logs = {0: logs_a[:, 0, :], 1: logs_a[:, 1, :], 3: logs_a[:, 2, :], 2: logs_b[:]}
+        for t in (0, 1, LAST):
+            nc.scalar.activation(logs[t], both[t][:], ACT.Ln)
+        for cols, ents in halves:
+            nc.scalar.activation(logs_b[:, cols], both[2][:, cols], ACT.Ln)
         warm2 = sb("warm2", [P, 1], F32)
-        nc.scalar.activation(warm2[:], logs[:, order[-1], 0:1], ACT.Silu)
+        nc.scalar.activation(warm2[:], logs_b[:, S - 1 : S], ACT.Silu)
         logit = sb("logit", [P, PACK, S], F32)
-        for t in order:
-            nc.vector.scalar_tensor_tensor(logit[:, t, :], score[t][:], SCORE, logs[:, t, :], ALU.mult, ALU.subtract)
-        ws_dealt = sb("ws_dealt", [P, S], U8, after="second")
+        for n in (0, 1, 2, 4, 3):
+            t, cols = parts[n]
+            nc.vector.scalar_tensor_tensor(logit[:, t, cols], score[n], SCORE, logs[t][:, cols], ALU.mult, ALU.subtract)
+        ws_dealt = sb("ws_dealt", [P, S], U8, after="logs_b")
         nc.vector.tensor_copy(
             ws_dealt[:].rearrange("p (t m) -> p m t", t=PACK), ws_raw[:].rearrange("p (m t) -> p m t", t=PACK)
         )
-        old_m = sb("old_m", [P, S], F32, after="first2")
-        nc.vector.tensor_scalar(old_m[:], page[0][:].indirect(n3_t[:]), -0.5, 0.0, ALU.mult, ALU.add)
 
-        hsum = [psum.tile([P, S], F32, name="hsum%d" % t) for t in range(PACK)]
-        share = [sb("share%d" % a, [P, HALF, PACK], F32, after=("warm2", None)[a]) for a in range(2)]
-        zb = [sb("zb%d" % a, [P, HALF, PACK], BF16) for a in range(2)]
-        z_codes = [sb("z_codes%d" % a, [P, HALF], U32) for a in range(2)]
-        z_scales = [sb("z_scales%d" % a, [P, HALF], U8) for a in range(2)]
-        gain_b = gain[:].unsqueeze(1).broadcast_to([P, HALF, PACK])
-        for a in range(2):
-            cols = slice(HALF * a, HALF * (a + 1))
+        hsum = [psum.tile([P, S], F32, name="hsum%d" % n, tag="score%d" % n) for n in range(len(parts))]
+
+        def sums(t, cols):
+            n = t + 1 if t else cols.start // HALF
+            return hsum[n][:, cols]
+
+        share = [sb("share%d" % a, [P, PIECE, PACK], F32, after="warm2" if a == 0 else None) for a in range(S // PIECE)]
+        zb = [sb("zb%d" % a, [P, PIECE, PACK], BF16) for a in range(S // PIECE)]
+        z_codes = [sb("z_codes%d" % a, [P, PIECE], U32) for a in range(S // PIECE)]
+        z_scales = [sb("z_scales%d" % a, [P, PIECE], U8) for a in range(S // PIECE)]
+        gain_b = gain[:].unsqueeze(1).broadcast_to([P, PIECE, PACK])
+        for a in range(S // PIECE):
+            cols = slice(PIECE * a, PIECE * (a + 1))
             nc.scalar.activation(
                 share[a][:].rearrange("p (c i) t -> p c t i", i=4),
                 logit[:, :, cols].rearrange("p t (c i) -> p c t i", i=4), ACT.Tanh, scale=0.5,
             )
-        for a in range(2):
-            cols = slice(HALF * a, HALF * (a + 1))
+        for a in range(S // PIECE):
             nc.vector.scalar_tensor_tensor(zb[a][:], share[a][:], 1.0, gain_b, ALU.add, ALU.mult)
-            nc.vector.quantize_mx(
-                out=z_codes[a][:].bitcast(FP8X4), scales=z_scales[a][:], in_=zb[a][:].rearrange("p j t -> p (j t)")
-            )
-            for t in range(PACK):
-                nc.tensor.matmul_mx(
-                    out=hsum[t][:, cols], lhsT=w_dealt[:, 2 * P * t : 2 * P * (t + 1)].bitcast(FP4X4),
-                    lhsT_scale=ws_dealt[:, P * t : P * (t + 1)],
-                    rhs=z_codes[a][:].bitcast(FP8X4), rhs_scale=z_scales[a][:], start=True, stop=True,
+            for b in ([a - 1] if a else []) + ([a] if a == S // PIECE - 1 else []):
+                cols = slice(PIECE * b, PIECE * (b + 1))
+                nc.vector.quantize_mx(
+                    out=z_codes[b][:].bitcast(FP8X4), scales=z_scales[b][:], in_=zb[b][:].rearrange("p j t -> p (j t)")
                 )
+                for t in range(PACK):
+                    nc.tensor.matmul_mx(
+                        out=sums(t, cols), lhsT=w_dealt[:, 2 * P * t : 2 * P * (t + 1)].bitcast(FP4X4),
+                        lhsT_scale=ws_dealt[:, P * t : P * (t + 1)],
+                        rhs=z_codes[b][:].bitcast(FP8X4), rhs_scale=z_scales[b][:], start=True, stop=True,
+                    )
 
         out_rows = out_0.rearrange("(p t) u -> p t u", t=PACK)
         th = [sb("th%d" % t, [P, S], F32) for t in range(PACK)]
@@ -176,43 +195,65 @@ def tile_picked_keysharepaget_none_po_kernel(
         fresh = [sb("fresh%d" % t, [P, S], F32) for t in range(PACK)]
         kept = [sb("kept%d" % t, [P, S], F32) for t in range(PACK)]
         yb = [sb("yb%d" % a, [P, SLOTS // 2, PACK], BF16) for a in range(2)]
-        for a in range(2):
-            cols = slice(HALF * a, HALF * (a + 1))
-            nc.scalar.activation(th[0][:, cols], hsum[0][:, cols], ACT.Tanh, scale=0.5)
-            nc.scalar.activation(fresh[0][:, cols], hsum[0][:, cols], ACT.Silu)
-        for t in range(1, PACK):
-            nc.scalar.activation(th[t][:], hsum[t][:], ACT.Tanh, scale=0.5)
-            nc.scalar.activation(stay[t][:], th[t][:], ACT.Copy, scale=-0.5, bias=0.5)
-            nc.scalar.activation(fresh[t][:], hsum[t][:], ACT.Silu)
-        for t in range(PACK):
-            if t == 0:
-                for a in range(2):
-                    cols = slice(HALF * a, HALF * (a + 1))
-                    nc.vector.scalar_tensor_tensor(kept[0][:, cols], th[0][:, cols], -1.0, old_m[:, cols], ALU.add, ALU.mult)
-                    nc.vector.tensor_tensor(
-                        page[0][:].indirect(n3_t[:, 16 * a : 16 * (a + 1)]), kept[0][:, cols], fresh[0][:, cols], ALU.add
-                    )
-            else:
-                nc.vector.tensor_tensor(kept[t][:], page[t][:].indirect(n3_t[:]), stay[t][:], ALU.mult)
-                nc.vector.tensor_tensor(page[t][:].indirect(n3_t[:]), kept[t][:], fresh[t][:], ALU.add)
+        def gate(t, cols):
+            nc.scalar.activation(th[t][:, cols], sums(t, cols), ACT.Tanh, scale=0.5)
+            nc.scalar.activation(stay[t][:, cols], th[t][:, cols], ACT.Copy, scale=-0.5, bias=0.5)
+
+        def value(t, cols):
+            nc.scalar.activation(fresh[t][:, cols], sums(t, cols), ACT.Silu)
+
+        def fetch(t, cols, ents):
+            nc.vector.tensor_tensor(kept[t][:, cols], page[t][:].indirect(n3_t[:, ents]), stay[t][:, cols], ALU.mult)
+
+        def put(t, cols, ents):
+            nc.vector.tensor_tensor(page[t][:].indirect(n3_t[:, ents]), kept[t][:, cols], fresh[t][:, cols], ALU.add)
+
+        def hand_out(t):
             nc.sync.dma_start(out_rows[:, t, :], page[t][:])
             for a in range(2):
                 src = page[t][:, a * SLOTS // 2 : (a + 1) * SLOTS // 2]
                 if t == LAST and a == 0:
-                    nc.vector.tensor_copy(yb[a][:, :, t], src)
+                    for b in range(2):
+                        quarter = slice(b * SLOTS // 4, (b + 1) * SLOTS // 4)
+                        nc.vector.tensor_copy(yb[a][:, quarter, t], src[:, quarter])
                 elif t == LAST - 1 and a == 0:
                     nc.scalar.copy(yb[a][:, :, t:], src.unsqueeze(2).broadcast_to([P, SLOTS // 2, 2]))
                 else:
                     nc.scalar.copy(yb[a][:, :, t], src)
+
+        every = slice(0, S // 16)
+        for cols, ents in halves:
+            gate(0, cols)
+        value(0, halves[0][0])
+        gate(1, whole)
+        value(0, halves[1][0])
+        for t in range(1, PACK):
+            if t < LAST:
+                gate(t + 1, whole)
+            value(t, whole)
+        for cols, ents in halves:
+            fetch(0, cols, ents)
+        put(0, *halves[0])
+        fetch(1, whole, every)
+        put(0, *halves[1])
+        hand_out(0)
+        for t in range(1, PACK):
+            if t < LAST:
+                fetch(t + 1, whole, every)
+            put(t, whole, every)
+            hand_out(t)
 
         y_codes = [sb("y_codes%d" % a, [P, SLOTS // 2], U32) for a in range(2)]
         y_scales = sb("y_scales", [P, SLOTS], U8)
         words_out = out_1[0].rearrange("p n t -> p (n t)").bitcast(I32)
         for a in range(2):
             cols = slice(a * SLOTS // 2, (a + 1) * SLOTS // 2)
-            nc.vector.quantize_mx(
-                out=y_codes[a][:].bitcast(FP8X4), scales=y_scales[:, cols], in_=yb[a][:].rearrange("p j t -> p (j t)")
-            )
+            width = SLOTS // 4 if a == 0 else SLOTS // 2
+            for b in range(0, SLOTS // 2, width):
+                nc.vector.quantize_mx(
+                    out=y_codes[a][:, b : b + width].bitcast(FP8X4), scales=y_scales[:, cols][:, b : b + width],
+                    in_=yb[a][:, b : b + width, :].rearrange("p j t -> p (j t)"),
+                )
             nc.sync.dma_start(words_out[:, cols], y_codes[a][:].bitcast(I32))
         scales_out = out_2[0].bitcast(I32)
         for q in range(4):

@@ -15,10 +15,12 @@ ALU = mybir.AluOpType
 
 P = 128
 PACK = 4
+LAST = PACK - 1
+SCALE_ROWS = 16
 TABLE = 2048
 S = 512
+LIST_COLS = S // 16
 SLOTS = 1024
-HALF = S // 2
 PIECE = S // 4
 SCORE = 0.0625 * 0.5
 FLOPS = 2 * 2 * 512 * 512 * 512
@@ -33,174 +35,193 @@ def tile_picked_keysharepaget_none_po_kernel(
         keep = ctx.enter_context(tc.tile_pool(name="keep", bufs=1))
         psum = ctx.enter_context(tc.psum_pool(name="psum", bufs=1))
 
-        def sb(name, shape, dtype, after=None):
-            return keep.tile(shape, dtype, name=name, tag=after or name, align_bytes=64)
+        def sbuf(name, shape, dtype, on=None):
+            return keep.tile(shape, dtype, name=name, tag=on or name, align_bytes=64)
 
-        kidx_t = sb("kidx_t", [P, S // 16], U16)
-        offs_t = sb("offs_t", [P, S // 16], U16)
-        n1_t = sb("n1_t", [P, S // 16], U16)
-        n2_t = sb("n2_t", [P, S // 16], U16)
-        n3_t = sb("n3_t", [P, S // 16], U16)
-        ds_tab = sb("ds_tab", [P, TABLE], U8)
-        xs_tab = sb("xs_tab", [P, TABLE], U8)
-        win = [sb("win%d" % t, [P, S if t < PACK - 1 else 2 * S], F32) for t in range(PACK)]
-        halves = [(slice(HALF * a, HALF * (a + 1)), slice(16 * a, 16 * (a + 1))) for a in range(2)]
-        warm_in = sb("warm_in", [P, 1], F32)
-        warm = sb("warm", [P, 1], F32)
-        nc.gpsimd.memset(warm_in[:], 0.0)
-        nc.scalar.activation(warm[:], warm_in[:], ACT.Exp)
+        def eightfold(scales):
+            rows = scales[0].bitcast(I32)
+            return rows.unsqueeze(1).broadcast_to([SCALE_ROWS, P // SCALE_ROWS, rows.shape[1]])
 
-        nc.vector.memset(ds_tab[:].bitcast(I32), 0)
-        nc.vector.memset(xs_tab[:].bitcast(I32), 0)
-        nc.vector.memset(win[PACK - 1][:, S:], 0.0)
+        def place_scale_rows(plane):
+            for j in range(1, 4):
+                nc.scalar.dma_start(plane[:].bitcast(I32)[j:P:32, :], plane[:].bitcast(I32)[8 * j : P : 32, :])
 
+        whole = (slice(0, S), slice(0, LIST_COLS))
+        halves = [
+            (slice(a * S // 2, (a + 1) * S // 2), slice(a * LIST_COLS // 2, (a + 1) * LIST_COLS // 2)) for a in range(2)
+        ]
+
+        zero = sbuf("zero", [P, 1], F32)
+        exp_preload = sbuf("exp_preload", [P, 1], F32)
+        nc.gpsimd.memset(zero[:], 0.0)
+        nc.scalar.activation(exp_preload[:], zero[:], ACT.Exp)
+
+        window = [sbuf("window%d" % t, [P, S if t < LAST else 2 * S], F32) for t in range(PACK)]
+        nc.vector.memset(window[LAST][:, S:], 0.0)
+
+        kidx_t = sbuf("kidx_t", [P, LIST_COLS], U16)
+        offs_t = sbuf("offs_t", [P, LIST_COLS], U16)
+        n1_t = sbuf("n1_t", [P, LIST_COLS], U16)
+        n2_t = sbuf("n2_t", [P, LIST_COLS], U16)
+        n3_t = sbuf("n3_t", [P, LIST_COLS], U16)
+        ds_table = sbuf("ds_table", [P, TABLE], U8)
+        xs_table = sbuf("xs_table", [P, TABLE], U8)
+        d_table = sbuf("d_table", [P, TABLE], I32)
+        x_table = sbuf("x_table", [P, TABLE], I32)
         nc.sync.dma_start(kidx_t[:], kidx)
-        ds_rows = d_scales[0].bitcast(I32)
-        nc.sync.dma_start(ds_tab[:].bitcast(I32)[0:P:8, :], ds_rows)
-        nc.sync.dma_start(xs_tab[:].bitcast(I32)[0:P:8, :], x_scales[0].bitcast(I32))
+        nc.sync.dma_start(ds_table[:].bitcast(I32), eightfold(d_scales))
         nc.sync.dma_start(offs_t[:], offs)
+        nc.sync.dma_start(xs_table[:].bitcast(I32), eightfold(x_scales))
+        nc.sync.dma_start(d_table[:], d_words[0].rearrange("p n t -> p (n t)").bitcast(I32))
+        nc.sync.dma_start(x_table[:], x_words[0].rearrange("p n t -> p (n t)").bitcast(I32))
         nc.sync.dma_start(n1_t[:], n1)
         nc.sync.dma_start(n2_t[:], n2)
         nc.sync.dma_start(n3_t[:], n3)
-        d_tab = sb("d_tab", [P, TABLE], I32, after="warm_in")
-        x_tab = sb("x_tab", [P, TABLE], I32, after="warm")
-        nc.sync.dma_start(d_tab[:], d_words[0].rearrange("p n t -> p (n t)").bitcast(I32))
-        nc.sync.dma_start(x_tab[:], x_words[0].rearrange("p n t -> p (n t)").bitcast(I32))
-        w_raw = sb("w_raw", [P, 2 * S], U8)
-        ws_raw = sb("ws_raw", [P, S], U8)
-        gain = sb("gain", [P, PACK], F32)
+        w_raw = sbuf("w_raw", [P, 2 * S], U8)
+        ws_raw = sbuf("ws_raw", [P, S], U8)
+        gain = sbuf("gain", [P, PACK], F32)
         nc.gpsimd.dma_start(w_raw[:].bitcast(I32), w1_words[0].bitcast(I32))
-        nc.gpsimd.memset(ws_raw[:].bitcast(I32), 0)
-        ws_rows = w1_scales[0].bitcast(I32)
-        for q in range(4):
-            nc.gpsimd.dma_start(ws_raw[:].bitcast(I32)[32 * q : 32 * q + 4, :], ws_rows[4 * q : 4 * q + 4, :])
+        nc.gpsimd.dma_start(ws_raw[:].bitcast(I32), eightfold(w1_scales))
         nc.gpsimd.dma_start(gain[:], gn.rearrange("(p t) o -> p (t o)", t=PACK))
 
-
-        ds_got = sb("ds_got", [P, S], U8)
-        xs_got = sb("xs_got", [P, S], U8)
-        planes = sb("planes", [P, 2 * S], U8)
-        nc.vector.tensor_copy(ds_got[:], ds_tab[:].indirect(kidx_t[:]))
-        nc.vector.tensor_copy(xs_got[:], xs_tab[:].indirect(offs_t[:]))
+        ds_got = sbuf("ds_got", [P, S], U8)
+        xs_got = sbuf("xs_got", [P, S], U8)
+        score_scales = sbuf("score_scales", [P, 2 * S], U8)
+        nc.vector.tensor_copy(ds_got[:], ds_table[:].indirect(kidx_t[:]))
+        nc.vector.tensor_copy(xs_got[:], xs_table[:].indirect(offs_t[:]))
         nc.vector.tensor_copy(
-            planes[:, :S].rearrange("p (t m) -> p m t", t=PACK), ds_got[:].rearrange("p (m t) -> p m t", t=PACK)
+            score_scales[:, :S].rearrange("p (t m) -> p m t", t=PACK), ds_got[:].rearrange("p (m t) -> p m t", t=PACK)
         )
-        nc.vector.tensor_copy(planes[:, S:].bitcast(I32), xs_got[:].bitcast(I32))
-        for j in range(1, 4):
-            nc.scalar.dma_start(planes[:].bitcast(I32)[j:P:32, :], planes[:].bitcast(I32)[8 * j : P : 32, :])
-        d_got = sb("d_got", [P, S], U32, after="ds_got")
-        d_dealt = sb("d_dealt", [P, S], U32)
+        nc.vector.tensor_copy(score_scales[:, S:].bitcast(I32), xs_got[:].bitcast(I32))
+        place_scale_rows(score_scales)
+
+        d_got = sbuf("d_got", [P, S], U32, on="ds_got")
+        d_dealt = sbuf("d_dealt", [P, S], U32)
+        x_got = sbuf("x_got", [P, S], U32)
         for cols, ents in halves:
-            nc.vector.tensor_copy(d_got[:, cols], d_tab[:].bitcast(U32).indirect(kidx_t[:, ents]))
+            nc.vector.tensor_copy(d_got[:, cols], d_table[:].bitcast(U32).indirect(kidx_t[:, ents]))
         for a, (cols, ents) in enumerate(halves):
             nc.vector.tensor_copy(
-                d_dealt[:].rearrange("p (t m) -> p m t", t=PACK)[:, 64 * a : 64 * (a + 1), :],
+                d_dealt[:].rearrange("p (t m) -> p m t", t=PACK)[:, a * P // 2 : (a + 1) * P // 2, :],
                 d_got[:, cols].rearrange("p (m t) -> p m t", t=PACK),
             )
-        x_got = sb("x_got", [P, S], U32)
         for cols, ents in halves:
-            nc.vector.tensor_copy(x_got[:, cols], x_tab[:].bitcast(U32).indirect(offs_t[:, ents]))
+            nc.vector.tensor_copy(x_got[:, cols], x_table[:].bitcast(U32).indirect(offs_t[:, ents]))
 
-        whole = slice(0, S)
-        parts = [(0, cols) for cols, ents in halves] + [(t, whole) for t in range(1, PACK)]
+        parts = [(0, cols) for cols, ents in halves] + [(t, whole[0]) for t in range(1, PACK)]
         score = []
         for n, (t, cols) in enumerate(parts):
-            bank = psum.tile([P, S], F32, name="score%d" % n)
+            bank = psum.tile([P, S], F32, name="score%d" % n, tag="bank%d" % n)
             score.append(bank[:, cols])
             keys = slice(P * t, P * (t + 1))
             nc.tensor.matmul_mx(
-                out=score[n], lhsT=d_dealt[:, keys].bitcast(FP8X4), lhsT_scale=planes[:, keys],
-                rhs=x_got[:, cols].bitcast(FP8X4), rhs_scale=planes[:, S:][:, cols], start=True, stop=True,
+                out=score[n], lhsT=d_dealt[:, keys].bitcast(FP8X4), lhsT_scale=score_scales[:, keys],
+                rhs=x_got[:, cols].bitcast(FP8X4), rhs_scale=score_scales[:, S:][:, cols], start=True, stop=True,
             )
 
         mem_rows = mem.rearrange("(p t) u -> p t u", t=PACK)
-        page = [sb("page%d" % t, [P, SLOTS], F32, after=a) for t, a in enumerate(("warm_in", "ds_got", "x_got", "planes"))]
+        page = [
+            sbuf("page%d" % t, [P, SLOTS], F32, on=tag)
+            for t, tag in enumerate(("d_table", "ds_got", "x_got", "score_scales"))
+        ]
         for t in range(PACK):
             nc.sync.dma_start(page[t][:], mem_rows[:, t, :])
 
-        w_dealt = sb("w_dealt", [P, 2 * S], U8, after="warm")
+        w_dealt = sbuf("w_dealt", [P, 2 * S], U8, on="x_table")
         nc.vector.tensor_copy(
             w_dealt[:].rearrange("p (t m b) -> p m t b", t=PACK, b=2),
             w_raw[:].rearrange("p (m t b) -> p m t b", t=PACK, b=2),
         )
-
-        LAST = PACK - 1
-        first = [sb("first%d" % t, [P, S], F32) for t in range(PACK)]
-        second = sb("second", [P, S], F32)
-        both = {t: sb("both%d" % t, [P, S], F32) for t in (0, 1, LAST)}
-        for n, (t, cols) in enumerate(parts):
-            nc.scalar.activation(win[t][:, cols], score[n], ACT.Exp if t < LAST else ACT.Copy, scale=SCORE)
-        nc.scalar.activation(first[LAST][:], win[LAST][:].indirect(n1_t[:]), ACT.Exp)
-        nc.scalar.activation(second[:], win[LAST][:].indirect(n2_t[:]), ACT.Exp)
-        for t in range(LAST):
-            for cols, ents in halves:
-                nc.vector.tensor_copy(first[t][:, cols], win[t][:].indirect(n1_t[:, ents]))
-            if t == LAST - 1:
-                nc.vector.tensor_tensor(both[LAST][:], first[LAST][:], second[:], ALU.add)
-                both[t] = sb("both%d" % t, [P, S], F32, after="second")
-            for cols, ents in halves:
-                nc.vector.tensor_tensor(both[t][:, cols], win[t][:].indirect(n2_t[:, ents]), first[t][:, cols], ALU.add)
-        logs_a = sb("logs_a", [P, LAST, S], F32, after="win3")
-        logs_b = sb("logs_b", [P, S], F32)
-        logs = {0: logs_a[:, 0, :], 1: logs_a[:, 1, :], 3: logs_a[:, 2, :], 2: logs_b[:]}
-        for t in (0, 1, LAST):
-            nc.scalar.activation(logs[t], both[t][:], ACT.Ln)
-        for cols, ents in halves:
-            nc.scalar.activation(logs_b[:, cols], both[2][:, cols], ACT.Ln)
-        warm2 = sb("warm2", [P, 1], F32)
-        nc.scalar.activation(warm2[:], logs_b[:, S - 1 : S], ACT.Silu)
-        logit = sb("logit", [P, PACK, S], F32)
-        for n in (0, 1, 2, 4, 3):
-            t, cols = parts[n]
-            nc.vector.scalar_tensor_tensor(logit[:, t, cols], score[n], SCORE, logs[t][:, cols], ALU.mult, ALU.subtract)
-        ws_dealt = sb("ws_dealt", [P, S], U8, after="logs_b")
+        ws_dealt = sbuf("ws_dealt", [P, S], U8, on="w_raw")
         nc.vector.tensor_copy(
             ws_dealt[:].rearrange("p (t m) -> p m t", t=PACK), ws_raw[:].rearrange("p (m t) -> p m t", t=PACK)
         )
+        place_scale_rows(ws_dealt)
 
-        hsum = [psum.tile([P, S], F32, name="hsum%d" % n, tag="score%d" % n) for n in range(len(parts))]
+        at_n1 = [sbuf("at_n1_%d" % t, [P, S], F32) for t in range(PACK)]
+        at_n2_last = sbuf("at_n2_last", [P, S], F32)
+        q = {t: sbuf("q%d" % t, [P, S], F32) for t in range(PACK) if t != LAST - 1}
+        for n, (t, cols) in enumerate(parts):
+            nc.scalar.activation(window[t][:, cols], score[n], ACT.Exp if t < LAST else ACT.Copy, scale=SCORE)
+        nc.scalar.activation(at_n1[LAST][:], window[LAST][:].indirect(n1_t[:]), ACT.Exp)
+        nc.scalar.activation(at_n2_last[:], window[LAST][:].indirect(n2_t[:]), ACT.Exp)
+        for t in range(LAST):
+            for cols, ents in halves:
+                nc.vector.tensor_copy(at_n1[t][:, cols], window[t][:].indirect(n1_t[:, ents]))
+            if t == LAST - 1:
+                nc.vector.tensor_tensor(q[LAST][:], at_n1[LAST][:], at_n2_last[:], ALU.add)
+                q[t] = sbuf("q%d" % t, [P, S], F32, on="at_n2_last")
+            for cols, ents in halves:
+                nc.vector.tensor_tensor(q[t][:, cols], window[t][:].indirect(n2_t[:, ents]), at_n1[t][:, cols], ALU.add)
 
-        def sums(t, cols):
-            n = t + 1 if t else cols.start // HALF
-            return hsum[n][:, cols]
+        early = [t for t in range(PACK) if t != LAST - 1]
+        ln_early = sbuf("ln_early", [P, len(early), S], F32, on="window%d" % LAST)
+        ln_late = sbuf("ln_late", [P, S], F32)
+        ln_q = {t: ln_early[:, i, :] for i, t in enumerate(early)}
+        ln_q[LAST - 1] = ln_late[:]
+        for t in early:
+            nc.scalar.activation(ln_q[t], q[t][:], ACT.Ln)
+        for cols, ents in halves:
+            nc.scalar.activation(ln_late[:, cols], q[LAST - 1][:, cols], ACT.Ln)
+        silu_preload = sbuf("silu_preload", [P, 1], F32)
+        nc.scalar.activation(silu_preload[:], ln_late[:, S - 1 : S], ACT.Silu)
+        logit = sbuf("logit", [P, PACK, S], F32)
+        for n in sorted(range(len(parts)), key=lambda n: parts[n][0] == LAST - 1):
+            t, cols = parts[n]
+            nc.vector.scalar_tensor_tensor(logit[:, t, cols], score[n], SCORE, ln_q[t][:, cols], ALU.mult, ALU.subtract)
 
-        share = [sb("share%d" % a, [P, PIECE, PACK], F32, after="warm2" if a == 0 else None) for a in range(S // PIECE)]
-        zb = [sb("zb%d" % a, [P, PIECE, PACK], BF16) for a in range(S // PIECE)]
-        z_codes = [sb("z_codes%d" % a, [P, PIECE], U32) for a in range(S // PIECE)]
-        z_scales = [sb("z_scales%d" % a, [P, PIECE], U8) for a in range(S // PIECE)]
-        gain_b = gain[:].unsqueeze(1).broadcast_to([P, PIECE, PACK])
-        for a in range(S // PIECE):
-            cols = slice(PIECE * a, PIECE * (a + 1))
+        h_bank = [psum.tile([P, S], F32, name="h%d" % n, tag="bank%d" % n) for n in range(len(parts))]
+
+        def h_at(t, cols):
+            return h_bank[t + 1 if t else cols.start // (S // 2)][:, cols]
+
+        pieces = [slice(c, c + PIECE) for c in range(0, S, PIECE)]
+        share = [
+            sbuf("share%d" % a, [P, PIECE, PACK], F32, on="silu_preload" if a == 0 else None)
+            for a in range(len(pieces))
+        ]
+        z = [sbuf("z%d" % a, [P, PIECE, PACK], BF16) for a in range(len(pieces))]
+        z_words = [sbuf("z_words%d" % a, [P, PIECE], U32) for a in range(len(pieces))]
+        z_scales = [sbuf("z_scales%d" % a, [P, PIECE], U8) for a in range(len(pieces))]
+        gain_by_column = gain[:].unsqueeze(1).broadcast_to([P, PIECE, PACK])
+
+        def multiply(a):
+            nc.vector.quantize_mx(
+                out=z_words[a][:].bitcast(FP8X4), scales=z_scales[a][:], in_=z[a][:].rearrange("p j t -> p (j t)")
+            )
+            for t in range(PACK):
+                nc.tensor.matmul_mx(
+                    out=h_at(t, pieces[a]), lhsT=w_dealt[:, 2 * P * t : 2 * P * (t + 1)].bitcast(FP4X4),
+                    lhsT_scale=ws_dealt[:, P * t : P * (t + 1)],
+                    rhs=z_words[a][:].bitcast(FP8X4), rhs_scale=z_scales[a][:], start=True, stop=True,
+                )
+
+        for a, cols in enumerate(pieces):
             nc.scalar.activation(
                 share[a][:].rearrange("p (c i) t -> p c t i", i=4),
                 logit[:, :, cols].rearrange("p t (c i) -> p c t i", i=4), ACT.Tanh, scale=0.5,
             )
-        for a in range(S // PIECE):
-            nc.vector.scalar_tensor_tensor(zb[a][:], share[a][:], 1.0, gain_b, ALU.add, ALU.mult)
-            for b in ([a - 1] if a else []) + ([a] if a == S // PIECE - 1 else []):
-                cols = slice(PIECE * b, PIECE * (b + 1))
-                nc.vector.quantize_mx(
-                    out=z_codes[b][:].bitcast(FP8X4), scales=z_scales[b][:], in_=zb[b][:].rearrange("p j t -> p (j t)")
-                )
-                for t in range(PACK):
-                    nc.tensor.matmul_mx(
-                        out=sums(t, cols), lhsT=w_dealt[:, 2 * P * t : 2 * P * (t + 1)].bitcast(FP4X4),
-                        lhsT_scale=ws_dealt[:, P * t : P * (t + 1)],
-                        rhs=z_codes[b][:].bitcast(FP8X4), rhs_scale=z_scales[b][:], start=True, stop=True,
-                    )
+        for a in range(len(pieces)):
+            nc.vector.scalar_tensor_tensor(z[a][:], share[a][:], 1.0, gain_by_column, ALU.add, ALU.mult)
+            if a:
+                multiply(a - 1)
+        multiply(len(pieces) - 1)
 
         out_rows = out_0.rearrange("(p t) u -> p t u", t=PACK)
-        th = [sb("th%d" % t, [P, S], F32) for t in range(PACK)]
-        stay = [sb("stay%d" % t, [P, S], F32) for t in range(PACK)]
-        fresh = [sb("fresh%d" % t, [P, S], F32) for t in range(PACK)]
-        kept = [sb("kept%d" % t, [P, S], F32) for t in range(PACK)]
-        yb = [sb("yb%d" % a, [P, SLOTS // 2, PACK], BF16) for a in range(2)]
-        def gate(t, cols):
-            nc.scalar.activation(th[t][:, cols], sums(t, cols), ACT.Tanh, scale=0.5)
-            nc.scalar.activation(stay[t][:, cols], th[t][:, cols], ACT.Copy, scale=-0.5, bias=0.5)
+        tanh_h = [sbuf("tanh_h%d" % t, [P, S], F32) for t in range(PACK)]
+        stay = [sbuf("stay%d" % t, [P, S], F32) for t in range(PACK)]
+        fresh = [sbuf("fresh%d" % t, [P, S], F32) for t in range(PACK)]
+        kept = [sbuf("kept%d" % t, [P, S], F32) for t in range(PACK)]
+        sides = [slice(0, SLOTS // 2), slice(SLOTS // 2, SLOTS)]
+        quarters = [slice(0, SLOTS // 4), slice(SLOTS // 4, SLOTS // 2)]
+        rounded = [sbuf("rounded%d" % a, [P, SLOTS // 2, PACK], BF16) for a in range(2)]
 
-        def value(t, cols):
-            nc.scalar.activation(fresh[t][:, cols], sums(t, cols), ACT.Silu)
+        def gate(t, cols, ents):
+            nc.scalar.activation(tanh_h[t][:, cols], h_at(t, cols), ACT.Tanh, scale=0.5)
+            nc.scalar.activation(stay[t][:, cols], tanh_h[t][:, cols], ACT.Copy, scale=-0.5, bias=0.5)
+
+        def value(t, cols, ents):
+            nc.scalar.activation(fresh[t][:, cols], h_at(t, cols), ACT.Silu)
 
         def fetch(t, cols, ents):
             nc.vector.tensor_tensor(kept[t][:, cols], page[t][:].indirect(n3_t[:, ents]), stay[t][:, cols], ALU.mult)
@@ -210,52 +231,42 @@ def tile_picked_keysharepaget_none_po_kernel(
 
         def hand_out(t):
             nc.sync.dma_start(out_rows[:, t, :], page[t][:])
-            for a in range(2):
-                src = page[t][:, a * SLOTS // 2 : (a + 1) * SLOTS // 2]
-                if t == LAST and a == 0:
-                    for b in range(2):
-                        quarter = slice(b * SLOTS // 4, (b + 1) * SLOTS // 4)
-                        nc.vector.tensor_copy(yb[a][:, quarter, t], src[:, quarter])
-                elif t == LAST - 1 and a == 0:
-                    nc.scalar.copy(yb[a][:, :, t:], src.unsqueeze(2).broadcast_to([P, SLOTS // 2, 2]))
-                else:
-                    nc.scalar.copy(yb[a][:, :, t], src)
+            left, right = page[t][:, sides[0]], page[t][:, sides[1]]
+            if t == LAST:
+                for cols in quarters:
+                    nc.vector.tensor_copy(rounded[0][:, cols, t], left[:, cols])
+            elif t == LAST - 1:
+                nc.scalar.copy(rounded[0][:, :, t:], left.unsqueeze(2).broadcast_to([P, SLOTS // 2, 2]))
+            else:
+                nc.scalar.copy(rounded[0][:, :, t], left)
+            nc.scalar.copy(rounded[1][:, :, t], right)
 
-        every = slice(0, S // 16)
-        for cols, ents in halves:
-            gate(0, cols)
-        value(0, halves[0][0])
-        gate(1, whole)
-        value(0, halves[1][0])
-        for t in range(1, PACK):
-            if t < LAST:
-                gate(t + 1, whole)
-            value(t, whole)
-        for cols, ents in halves:
-            fetch(0, cols, ents)
-        put(0, *halves[0])
-        fetch(1, whole, every)
-        put(0, *halves[1])
-        hand_out(0)
-        for t in range(1, PACK):
-            if t < LAST:
-                fetch(t + 1, whole, every)
-            put(t, whole, every)
-            hand_out(t)
+        steps = [(0, *halves[0]), (0, *halves[1])] + [(t, *whole) for t in range(1, PACK)]
+        for i, step in enumerate(steps):
+            gate(*step)
+            if i:
+                value(*steps[i - 1])
+        value(*steps[-1])
+        for i, step in enumerate(steps):
+            fetch(*step)
+            if i:
+                put(*steps[i - 1])
+            if i > 1:
+                hand_out(steps[i - 1][0])
+        put(*steps[-1])
+        hand_out(LAST)
 
-        y_codes = [sb("y_codes%d" % a, [P, SLOTS // 2], U32) for a in range(2)]
-        y_scales = sb("y_scales", [P, SLOTS], U8)
-        words_out = out_1[0].rearrange("p n t -> p (n t)").bitcast(I32)
-        for a in range(2):
-            cols = slice(a * SLOTS // 2, (a + 1) * SLOTS // 2)
-            width = SLOTS // 4 if a == 0 else SLOTS // 2
-            for b in range(0, SLOTS // 2, width):
+        out_words = [sbuf("out_words%d" % a, [P, SLOTS // 2], U32) for a in range(2)]
+        out_scales = sbuf("out_scales", [P, SLOTS], U8)
+        words_hbm = out_1[0].rearrange("p n t -> p (n t)").bitcast(I32)
+        for a, cuts in enumerate((quarters, [sides[0]])):
+            for cols in cuts:
                 nc.vector.quantize_mx(
-                    out=y_codes[a][:, b : b + width].bitcast(FP8X4), scales=y_scales[:, cols][:, b : b + width],
-                    in_=yb[a][:, b : b + width, :].rearrange("p j t -> p (j t)"),
+                    out=out_words[a][:, cols].bitcast(FP8X4), scales=out_scales[:, sides[a]][:, cols],
+                    in_=rounded[a][:, cols, :].rearrange("p j t -> p (j t)"),
                 )
-            nc.sync.dma_start(words_out[:, cols], y_codes[a][:].bitcast(I32))
-        scales_out = out_2[0].bitcast(I32)
-        for q in range(4):
-            eng = nc.scalar if q % 2 else nc.sync
-            eng.dma_start(scales_out[4 * q : 4 * q + 4, :], y_scales[:].bitcast(I32)[32 * q : 32 * q + 4, :])
+            nc.sync.dma_start(words_hbm[:, sides[a]], out_words[a][:].bitcast(I32))
+        scales_hbm = out_2[0].bitcast(I32)
+        for g in range(4):
+            queue = nc.scalar if g % 2 else nc.sync
+            queue.dma_start(scales_hbm[4 * g : 4 * g + 4, :], out_scales[:].bitcast(I32)[32 * g : 32 * g + 4, :])

@@ -90,7 +90,7 @@ def tile_picked_keysharepaget_none_po_kernel(
         nc.vector.tensor_copy(ds_got[:], ds_table[:].indirect(kidx_t[:]))
         nc.vector.tensor_copy(xs_got[:], xs_table[:].indirect(offs_t[:]))
         nc.vector.tensor_copy(
-            score_scales[:, :S].rearrange("p (t m) -> p m t", t=PACK), ds_got[:].rearrange("p (m t) -> p m t", t=PACK)
+            score_scales[:, :S].rearrange("p (t m) -> p t m", t=PACK), ds_got[:].rearrange("p (m t) -> p t m", t=PACK)
         )
         nc.vector.tensor_copy(score_scales[:, S:].bitcast(I32), xs_got[:].bitcast(I32))
         place_scale_rows(score_scales)
@@ -129,12 +129,12 @@ def tile_picked_keysharepaget_none_po_kernel(
 
         w_dealt = sbuf("w_dealt", [P, 2 * S], U8, on="x_table")
         nc.vector.tensor_copy(
-            w_dealt[:].rearrange("p (t m b) -> p m t b", t=PACK, b=2),
-            w_raw[:].rearrange("p (m t b) -> p m t b", t=PACK, b=2),
+            w_dealt[:].rearrange("p (t m b) -> p t m b", t=PACK, b=2),
+            w_raw[:].rearrange("p (m t b) -> p t m b", t=PACK, b=2),
         )
         ws_dealt = sbuf("ws_dealt", [P, S], U8, on="w_raw")
         nc.vector.tensor_copy(
-            ws_dealt[:].rearrange("p (t m) -> p m t", t=PACK), ws_raw[:].rearrange("p (m t) -> p m t", t=PACK)
+            ws_dealt[:].rearrange("p (t m) -> p t m", t=PACK), ws_raw[:].rearrange("p (m t) -> p t m", t=PACK)
         )
         place_scale_rows(ws_dealt)
 
@@ -169,6 +169,9 @@ def tile_picked_keysharepaget_none_po_kernel(
         for n in sorted(range(len(parts)), key=lambda n: parts[n][0] == LAST - 1):
             t, cols = parts[n]
             nc.vector.scalar_tensor_tensor(logit[:, t, cols], score[n], SCORE, ln_q[t][:, cols], ALU.mult, ALU.subtract)
+
+        old_first = sbuf("old_first", [P, S], F32, on="ln_late")
+        nc.vector.tensor_scalar(old_first[:], page[0][:].indirect(n3_t[:]), -0.5, 0.0, ALU.mult, ALU.add)
 
         h_bank = [psum.tile([P, S], F32, name="h%d" % n, tag="bank%d" % n) for n in range(len(parts))]
 
@@ -209,37 +212,44 @@ def tile_picked_keysharepaget_none_po_kernel(
 
         out_rows = out_0.rearrange("(p t) u -> p t u", t=PACK)
         tanh_h = [sbuf("tanh_h%d" % t, [P, S], F32) for t in range(PACK)]
-        stay = [sbuf("stay%d" % t, [P, S], F32) for t in range(PACK)]
+        stay = {t: sbuf("stay%d" % t, [P, S], F32) for t in range(1, PACK)}
         fresh = [sbuf("fresh%d" % t, [P, S], F32) for t in range(PACK)]
         kept = [sbuf("kept%d" % t, [P, S], F32) for t in range(PACK)]
-        sides = [slice(0, SLOTS // 2), slice(SLOTS // 2, SLOTS)]
-        quarters = [slice(0, SLOTS // 4), slice(SLOTS // 4, SLOTS // 2)]
-        rounded = [sbuf("rounded%d" % a, [P, SLOTS // 2, PACK], BF16) for a in range(2)]
+        quarters = [slice(c, c + SLOTS // 4) for c in range(0, SLOTS, SLOTS // 4)]
+        split = quarters[-1].start
+        rounded_left = sbuf("rounded_left", [P, split, PACK], BF16)
+        rounded_right = sbuf("rounded_right", [P, SLOTS - split, PACK], BF16)
 
         def gate(t, cols, ents):
             nc.scalar.activation(tanh_h[t][:, cols], h_at(t, cols), ACT.Tanh, scale=0.5)
-            nc.scalar.activation(stay[t][:, cols], tanh_h[t][:, cols], ACT.Copy, scale=-0.5, bias=0.5)
+            if t:
+                nc.scalar.activation(stay[t][:, cols], tanh_h[t][:, cols], ACT.Copy, scale=-0.5, bias=0.5)
 
         def value(t, cols, ents):
             nc.scalar.activation(fresh[t][:, cols], h_at(t, cols), ACT.Silu)
 
         def fetch(t, cols, ents):
-            nc.vector.tensor_tensor(kept[t][:, cols], page[t][:].indirect(n3_t[:, ents]), stay[t][:, cols], ALU.mult)
+            if t:
+                nc.vector.tensor_tensor(kept[t][:, cols], page[t][:].indirect(n3_t[:, ents]), stay[t][:, cols], ALU.mult)
+            else:
+                nc.vector.scalar_tensor_tensor(
+                    kept[t][:, cols], tanh_h[t][:, cols], -1.0, old_first[:, cols], ALU.add, ALU.mult
+                )
 
         def put(t, cols, ents):
             nc.vector.tensor_tensor(page[t][:].indirect(n3_t[:, ents]), kept[t][:, cols], fresh[t][:, cols], ALU.add)
 
         def hand_out(t):
             nc.sync.dma_start(out_rows[:, t, :], page[t][:])
-            left, right = page[t][:, sides[0]], page[t][:, sides[1]]
+            left, right = page[t][:, :split], page[t][:, split:]
             if t == LAST:
-                for cols in quarters:
-                    nc.vector.tensor_copy(rounded[0][:, cols, t], left[:, cols])
+                for cols in quarters[:-1]:
+                    nc.vector.tensor_copy(rounded_left[:, cols, t], left[:, cols])
             elif t == LAST - 1:
-                nc.scalar.copy(rounded[0][:, :, t:], left.unsqueeze(2).broadcast_to([P, SLOTS // 2, 2]))
+                nc.scalar.copy(rounded_left[:, :, t:], left.unsqueeze(2).broadcast_to([P, split, 2]))
             else:
-                nc.scalar.copy(rounded[0][:, :, t], left)
-            nc.scalar.copy(rounded[1][:, :, t], right)
+                nc.scalar.copy(rounded_left[:, :, t], left)
+            nc.scalar.copy(rounded_right[:, :, t], right)
 
         steps = [(0, *halves[0]), (0, *halves[1])] + [(t, *whole) for t in range(1, PACK)]
         for i, step in enumerate(steps):
@@ -259,13 +269,15 @@ def tile_picked_keysharepaget_none_po_kernel(
         out_words = [sbuf("out_words%d" % a, [P, SLOTS // 2], U32) for a in range(2)]
         out_scales = sbuf("out_scales", [P, SLOTS], U8)
         words_hbm = out_1[0].rearrange("p n t -> p (n t)").bitcast(I32)
-        for a, cuts in enumerate((quarters, [sides[0]])):
-            for cols in cuts:
-                nc.vector.quantize_mx(
-                    out=out_words[a][:, cols].bitcast(FP8X4), scales=out_scales[:, sides[a]][:, cols],
-                    in_=rounded[a][:, cols, :].rearrange("p j t -> p (j t)"),
-                )
-            nc.sync.dma_start(words_hbm[:, sides[a]], out_words[a][:].bitcast(I32))
+        for i, cols in enumerate(quarters):
+            source = rounded_left[:, cols, :] if cols.start < split else rounded_right[:]
+            words = out_words[i // 2]
+            nc.vector.quantize_mx(
+                out=words[:, quarters[i % 2]].bitcast(FP8X4), scales=out_scales[:, cols],
+                in_=source.rearrange("p j t -> p (j t)"),
+            )
+            if i % 2:
+                nc.sync.dma_start(words_hbm[:, quarters[i - 1].start : cols.stop], words[:].bitcast(I32))
         scales_hbm = out_2[0].bitcast(I32)
         for g in range(4):
             queue = nc.scalar if g % 2 else nc.sync

from contextlib import ExitStack

import concourse.mybir as mybir

F32 = mybir.dt.float32
BF16 = mybir.dt.bfloat16
I32 = mybir.dt.int32
U32 = mybir.dt.uint32
U16 = mybir.dt.uint16
U8 = mybir.dt.uint8
FP8X4 = mybir.dt.float8_e4m3fn_x4
FP4X4 = mybir.dt.float4_e2m1fn_x4
ACT = mybir.ActivationFunctionType
ALU = mybir.AluOpType

P = 128
PACK = 4
LAST = PACK - 1
SCALE_ROWS = 16
TABLE = 2048
S = 512
LIST_COLS = S // 16
SLOTS = 1024
PIECE = S // 4
SCORE = 0.0625 * 0.5
FLOPS = 2 * 2 * 512 * 512 * 512


def tile_picked_keysharepaget_none_po_kernel(
    tc, x_words, x_scales, d_words, d_scales, gn, w1_words, w1_scales, mem,
    offs, kidx, n1, n2, n3, out_0, out_1, out_2,
):
    nc = tc.nc
    with ExitStack() as ctx:
        keep = ctx.enter_context(tc.tile_pool(name="keep", bufs=1))
        psum = ctx.enter_context(tc.psum_pool(name="psum", bufs=1))

        def sbuf(name, shape, dtype, on=None):
            return keep.tile(shape, dtype, name=name, tag=on or name, align_bytes=64)

        def eightfold(scales):
            rows = scales[0].bitcast(I32)
            return rows.unsqueeze(1).broadcast_to([SCALE_ROWS, P // SCALE_ROWS, rows.shape[1]])

        def place_scale_rows(plane):
            for j in range(1, 4):
                nc.scalar.dma_start(plane[:].bitcast(I32)[j:P:32, :], plane[:].bitcast(I32)[8 * j : P : 32, :])

        whole = (slice(0, S), slice(0, LIST_COLS))
        halves = [
            (slice(a * S // 2, (a + 1) * S // 2), slice(a * LIST_COLS // 2, (a + 1) * LIST_COLS // 2)) for a in range(2)
        ]

        zero = sbuf("zero", [P, 1], F32)
        exp_preload = sbuf("exp_preload", [P, 1], F32)
        nc.gpsimd.memset(zero[:], 0.0)
        nc.scalar.activation(exp_preload[:], zero[:], ACT.Exp)

        window = [sbuf("window%d" % t, [P, S if t < LAST else 2 * S], F32) for t in range(PACK)]
        nc.vector.memset(window[LAST][:, S:], 0.0)

        kidx_t = sbuf("kidx_t", [P, LIST_COLS], U16)
        offs_t = sbuf("offs_t", [P, LIST_COLS], U16)
        n1_t = sbuf("n1_t", [P, LIST_COLS], U16)
        n2_t = sbuf("n2_t", [P, LIST_COLS], U16)
        n3_t = sbuf("n3_t", [P, LIST_COLS], U16)
        ds_table = sbuf("ds_table", [P, TABLE], U8)
        xs_table = sbuf("xs_table", [P, TABLE], U8)
        d_table = sbuf("d_table", [P, TABLE], I32)
        x_table = sbuf("x_table", [P, TABLE], I32)
        nc.sync.dma_start(kidx_t[:], kidx)
        nc.sync.dma_start(ds_table[:].bitcast(I32), eightfold(d_scales))
        nc.sync.dma_start(offs_t[:], offs)
        nc.sync.dma_start(xs_table[:].bitcast(I32), eightfold(x_scales))
        nc.sync.dma_start(d_table[:], d_words[0].rearrange("p n t -> p (n t)").bitcast(I32))
        nc.sync.dma_start(x_table[:], x_words[0].rearrange("p n t -> p (n t)").bitcast(I32))
        nc.sync.dma_start(n1_t[:], n1)
        nc.sync.dma_start(n2_t[:], n2)
        nc.sync.dma_start(n3_t[:], n3)
        w_raw = sbuf("w_raw", [P, 2 * S], U8)
        ws_raw = sbuf("ws_raw", [P, S], U8)
        gain = sbuf("gain", [P, PACK], F32)
        nc.gpsimd.dma_start(w_raw[:].bitcast(I32), w1_words[0].bitcast(I32))
        nc.gpsimd.dma_start(ws_raw[:].bitcast(I32), eightfold(w1_scales))
        nc.gpsimd.dma_start(gain[:], gn.rearrange("(p t) o -> p (t o)", t=PACK))

        ds_got = sbuf("ds_got", [P, S], U8)
        xs_got = sbuf("xs_got", [P, S], U8)
        score_scales = sbuf("score_scales", [P, 2 * S], U8)
        nc.vector.tensor_copy(ds_got[:], ds_table[:].indirect(kidx_t[:]))
        nc.vector.tensor_copy(xs_got[:], xs_table[:].indirect(offs_t[:]))
        nc.vector.tensor_copy(
            score_scales[:, :S].rearrange("p (t m) -> p t m", t=PACK), ds_got[:].rearrange("p (m t) -> p t m", t=PACK)
        )
        nc.vector.tensor_copy(score_scales[:, S:].bitcast(I32), xs_got[:].bitcast(I32))
        place_scale_rows(score_scales)

        d_got = sbuf("d_got", [P, S], U32, on="ds_got")
        d_dealt = sbuf("d_dealt", [P, S], U32)
        x_got = sbuf("x_got", [P, S], U32)
        for cols, ents in halves:
            nc.vector.tensor_copy(d_got[:, cols], d_table[:].bitcast(U32).indirect(kidx_t[:, ents]))
        for a, (cols, ents) in enumerate(halves):
            nc.vector.tensor_copy(
                d_dealt[:].rearrange("p (t m) -> p m t", t=PACK)[:, a * P // 2 : (a + 1) * P // 2, :],
                d_got[:, cols].rearrange("p (m t) -> p m t", t=PACK),
            )
        for cols, ents in halves:
            nc.vector.tensor_copy(x_got[:, cols], x_table[:].bitcast(U32).indirect(offs_t[:, ents]))

        parts = [(0, cols) for cols, ents in halves] + [(t, whole[0]) for t in range(1, PACK)]
        score = []
        for n, (t, cols) in enumerate(parts):
            bank = psum.tile([P, S], F32, name="score%d" % n, tag="bank%d" % n)
            score.append(bank[:, cols])
            keys = slice(P * t, P * (t + 1))
            nc.tensor.matmul_mx(
                out=score[n], lhsT=d_dealt[:, keys].bitcast(FP8X4), lhsT_scale=score_scales[:, keys],
                rhs=x_got[:, cols].bitcast(FP8X4), rhs_scale=score_scales[:, S:][:, cols], start=True, stop=True,
            )

        mem_rows = mem.rearrange("(p t) u -> p t u", t=PACK)
        page = [
            sbuf("page%d" % t, [P, SLOTS], F32, on=tag)
            for t, tag in enumerate(("d_table", "ds_got", "x_got", "score_scales"))
        ]
        for t in range(PACK):
            nc.sync.dma_start(page[t][:], mem_rows[:, t, :])

        w_dealt = sbuf("w_dealt", [P, 2 * S], U8, on="x_table")
        nc.vector.tensor_copy(
            w_dealt[:].rearrange("p (t m b) -> p t m b", t=PACK, b=2),
            w_raw[:].rearrange("p (m t b) -> p t m b", t=PACK, b=2),
        )
        ws_dealt = sbuf("ws_dealt", [P, S], U8, on="w_raw")
        nc.vector.tensor_copy(
            ws_dealt[:].rearrange("p (t m) -> p t m", t=PACK), ws_raw[:].rearrange("p (m t) -> p t m", t=PACK)
        )
        place_scale_rows(ws_dealt)

        at_n1 = [sbuf("at_n1_%d" % t, [P, S], F32) for t in range(PACK)]
        at_n2_last = sbuf("at_n2_last", [P, S], F32)
        q = {t: sbuf("q%d" % t, [P, S], F32) for t in range(PACK) if t != LAST - 1}
        for n, (t, cols) in enumerate(parts):
            nc.scalar.activation(window[t][:, cols], score[n], ACT.Exp if t < LAST else ACT.Copy, scale=SCORE)
        nc.scalar.activation(at_n1[LAST][:], window[LAST][:].indirect(n1_t[:]), ACT.Exp)
        nc.scalar.activation(at_n2_last[:], window[LAST][:].indirect(n2_t[:]), ACT.Exp)
        for t in range(LAST):
            for cols, ents in halves:
                nc.vector.tensor_copy(at_n1[t][:, cols], window[t][:].indirect(n1_t[:, ents]))
            if t == LAST - 1:
                nc.vector.tensor_tensor(q[LAST][:], at_n1[LAST][:], at_n2_last[:], ALU.add)
                q[t] = sbuf("q%d" % t, [P, S], F32, on="at_n2_last")
            for cols, ents in halves:
                nc.vector.tensor_tensor(q[t][:, cols], window[t][:].indirect(n2_t[:, ents]), at_n1[t][:, cols], ALU.add)

        early = [t for t in range(PACK) if t != LAST - 1]
        ln_early = sbuf("ln_early", [P, len(early), S], F32, on="window%d" % LAST)
        ln_late = sbuf("ln_late", [P, S], F32)
        ln_q = {t: ln_early[:, i, :] for i, t in enumerate(early)}
        ln_q[LAST - 1] = ln_late[:]
        for t in early:
            nc.scalar.activation(ln_q[t], q[t][:], ACT.Ln)
        for cols, ents in halves:
            nc.scalar.activation(ln_late[:, cols], q[LAST - 1][:, cols], ACT.Ln)
        silu_preload = sbuf("silu_preload", [P, 1], F32)
        nc.scalar.activation(silu_preload[:], ln_late[:, S - 1 : S], ACT.Silu)
        logit = sbuf("logit", [P, PACK, S], F32)
        for n in sorted(range(len(parts)), key=lambda n: parts[n][0] == LAST - 1):
            t, cols = parts[n]
            nc.vector.scalar_tensor_tensor(logit[:, t, cols], score[n], SCORE, ln_q[t][:, cols], ALU.mult, ALU.subtract)

        old_first = sbuf("old_first", [P, S], F32, on="ln_late")
        nc.vector.tensor_scalar(old_first[:], page[0][:].indirect(n3_t[:]), -0.5, 0.0, ALU.mult, ALU.add)

        h_bank = [psum.tile([P, S], F32, name="h%d" % n, tag="bank%d" % n) for n in range(len(parts))]

        def h_at(t, cols):
            return h_bank[t + 1 if t else cols.start // (S // 2)][:, cols]

        pieces = [slice(c, c + PIECE) for c in range(0, S, PIECE)]
        share = [
            sbuf("share%d" % a, [P, PIECE, PACK], F32, on="silu_preload" if a == 0 else None)
            for a in range(len(pieces))
        ]
        z = [sbuf("z%d" % a, [P, PIECE, PACK], BF16) for a in range(len(pieces))]
        z_words = [sbuf("z_words%d" % a, [P, PIECE], U32) for a in range(len(pieces))]
        z_scales = [sbuf("z_scales%d" % a, [P, PIECE], U8) for a in range(len(pieces))]
        gain_by_column = gain[:].unsqueeze(1).broadcast_to([P, PIECE, PACK])

        def multiply(a):
            nc.vector.quantize_mx(
                out=z_words[a][:].bitcast(FP8X4), scales=z_scales[a][:], in_=z[a][:].rearrange("p j t -> p (j t)")
            )
            for t in range(PACK):
                nc.tensor.matmul_mx(
                    out=h_at(t, pieces[a]), lhsT=w_dealt[:, 2 * P * t : 2 * P * (t + 1)].bitcast(FP4X4),
                    lhsT_scale=ws_dealt[:, P * t : P * (t + 1)],
                    rhs=z_words[a][:].bitcast(FP8X4), rhs_scale=z_scales[a][:], start=True, stop=True,
                )

        for a, cols in enumerate(pieces):
            nc.scalar.activation(
                share[a][:].rearrange("p (c i) t -> p c t i", i=4),
                logit[:, :, cols].rearrange("p t (c i) -> p c t i", i=4), ACT.Tanh, scale=0.5,
            )
        for a in range(len(pieces)):
            nc.vector.scalar_tensor_tensor(z[a][:], share[a][:], 1.0, gain_by_column, ALU.add, ALU.mult)
            if a:
                multiply(a - 1)
        multiply(len(pieces) - 1)

        out_rows = out_0.rearrange("(p t) u -> p t u", t=PACK)
        tanh_h = [sbuf("tanh_h%d" % t, [P, S], F32) for t in range(PACK)]
        stay = {t: sbuf("stay%d" % t, [P, S], F32) for t in range(1, PACK)}
        fresh = [sbuf("fresh%d" % t, [P, S], F32) for t in range(PACK)]
        kept = [sbuf("kept%d" % t, [P, S], F32) for t in range(PACK)]
        quarters = [slice(c, c + SLOTS // 4) for c in range(0, SLOTS, SLOTS // 4)]
        split = quarters[-1].start
        rounded_left = sbuf("rounded_left", [P, split, PACK], BF16)
        rounded_right = sbuf("rounded_right", [P, SLOTS - split, PACK], BF16)

        def gate(t, cols, ents):
            nc.scalar.activation(tanh_h[t][:, cols], h_at(t, cols), ACT.Tanh, scale=0.5)
            if t:
                nc.scalar.activation(stay[t][:, cols], tanh_h[t][:, cols], ACT.Copy, scale=-0.5, bias=0.5)

        def value(t, cols, ents):
            nc.scalar.activation(fresh[t][:, cols], h_at(t, cols), ACT.Silu)

        def fetch(t, cols, ents):
            if t:
                nc.vector.tensor_tensor(kept[t][:, cols], page[t][:].indirect(n3_t[:, ents]), stay[t][:, cols], ALU.mult)
            else:
                nc.vector.scalar_tensor_tensor(
                    kept[t][:, cols], tanh_h[t][:, cols], -1.0, old_first[:, cols], ALU.add, ALU.mult
                )

        def put(t, cols, ents):
            nc.vector.tensor_tensor(page[t][:].indirect(n3_t[:, ents]), kept[t][:, cols], fresh[t][:, cols], ALU.add)

        def hand_out(t):
            nc.sync.dma_start(out_rows[:, t, :], page[t][:])
            left, right = page[t][:, :split], page[t][:, split:]
            if t == LAST:
                for cols in quarters[:-1]:
                    nc.vector.tensor_copy(rounded_left[:, cols, t], left[:, cols])
            elif t == LAST - 1:
                nc.scalar.copy(rounded_left[:, :, t:], left.unsqueeze(2).broadcast_to([P, split, 2]))
            else:
                nc.scalar.copy(rounded_left[:, :, t], left)
            nc.scalar.copy(rounded_right[:, :, t], right)

        steps = [(0, *halves[0]), (0, *halves[1])] + [(t, *whole) for t in range(1, PACK)]
        for i, step in enumerate(steps):
            gate(*step)
            if i:
                value(*steps[i - 1])
        value(*steps[-1])
        for i, step in enumerate(steps):
            fetch(*step)
            if i:
                put(*steps[i - 1])
            if i > 1:
                hand_out(steps[i - 1][0])
        put(*steps[-1])
        hand_out(LAST)

        out_words = [sbuf("out_words%d" % a, [P, SLOTS // 2], U32) for a in range(2)]
        out_scales = sbuf("out_scales", [P, SLOTS], U8)
        words_hbm = out_1[0].rearrange("p n t -> p (n t)").bitcast(I32)
        for i, cols in enumerate(quarters):
            source = rounded_left[:, cols, :] if cols.start < split else rounded_right[:]
            words = out_words[i // 2]
            nc.vector.quantize_mx(
                out=words[:, quarters[i % 2]].bitcast(FP8X4), scales=out_scales[:, cols],
                in_=source.rearrange("p j t -> p (j t)"),
            )
            if i % 2:
                nc.sync.dma_start(words_hbm[:, quarters[i - 1].start : cols.stop], words[:].bitcast(I32))
        scales_hbm = out_2[0].bitcast(I32)
        for g in range(4):
            queue = nc.scalar if g % 2 else nc.sync
            queue.dma_start(scales_hbm[4 * g : 4 * g + 4, :], out_scales[:].bitcast(I32)[32 * g : 32 * g + 4, :])
